import numpy as np
import ml_dtypes


def mxq(x, axis, fmt="e4m3"):
    dtype, down = {"e4m3": (ml_dtypes.float8_e4m3fn, 7), "e5m2": (ml_dtypes.float8_e5m2, 14)}[fmt]
    v = np.moveaxis(np.asarray(x, np.float32).astype(ml_dtypes.bfloat16).astype(np.float64), axis, -1)
    blocks = v.reshape(v.shape[:-1] + (-1, 32))
    amax = np.abs(blocks).max(-1, keepdims=True)
    byte = np.maximum(np.where(amax > 0, np.frexp(amax)[1] - 1 + 127, 0) - down, 1)
    scale = np.exp2(byte - 127.0)
    codes = (blocks / scale).astype(np.float32).astype(dtype).astype(np.float64)
    return np.moveaxis((codes * scale).reshape(v.shape), -1, axis)


WIDE = False


def mx_kscale(k):
    if not WIDE:
        return np.ones(k)
    levels = np.array([10, -10, 5, -5, 0])
    if k % 512:
        return np.exp2(np.random.permutation(np.resize(levels, k // 32))).repeat(32)
    a = np.empty((k // 512, 16))
    for p in range(k // 512):
        a[p, :8] = np.random.permutation(np.resize(levels, 8))
        for g in range(8):
            far = levels[np.abs(levels - a[p, g]) >= 10]
            a[p, g + 8] = far[np.random.randint(len(far))]
    return np.exp2(a.ravel()).repeat(32)


def f64(x):
    return np.asarray(x).astype(np.float64)


def striped8(idx):
    return np.concatenate([v.reshape(-1, 16).T for v in idx]).astype(np.uint16)


def unstriped8(offs):
    return np.stack([offs[16 * g:16 * g + 16].T.reshape(-1) for g in range(8)]).astype(np.int64)


E2M1 = np.array([0.0, 0.5, 1.0, 1.5, 2.0, 3.0, 4.0, 6.0, -0.0, -0.5, -1.0, -1.5, -2.0, -3.0, -4.0, -6.0])


def pack_weight(w, fmt):
    k, n = w.shape
    w = f64(np.asarray(w, np.float32).astype(ml_dtypes.bfloat16)).reshape(k // 32, 32, n)
    amax = np.abs(w).max(1)
    if fmt == "e4m3":
        byte = np.frexp(amax)[1] - 1 + 127 - 7
    else:
        mant, ex = np.frexp(amax / 6.0)
        byte = np.where(mant > 0.5, ex, ex - 1) + 127
    byte = np.clip(np.where(amax > 0, byte, 1), 1, 254)
    scaled = (w * np.exp2(127.0 - byte)[:, None, :]).reshape(k, n).astype(np.float32)
    by_word = np.ascontiguousarray(scaled.reshape(k // 512, 128, 4, n).transpose(0, 1, 3, 2))
    if fmt == "e4m3":
        words = by_word.astype(ml_dtypes.float8_e4m3fn).view(np.uint8)
    else:
        c = by_word.astype(ml_dtypes.float4_e2m1fn).view(np.uint8) & 0xF
        words = (c[..., 0::2] | (c[..., 1::2] << 4)).reshape(k // 512, 128, 2 * n)
    return np.ascontiguousarray(words), np.ascontiguousarray(byte.astype(np.uint8).reshape(k // 512, 16, n))


def unpack_weight(words, scales, fmt):
    g, _, n = scales.shape
    words = np.ascontiguousarray(words).reshape(g, 128, n, -1)
    if fmt == "e4m3":
        vals = words.view(ml_dtypes.float8_e4m3fn).astype(np.float64)
    else:
        nib = np.empty((g, 128, n, 4), np.uint8)
        nib[..., 0::2] = words & 0xF
        nib[..., 1::2] = words >> 4
        vals = E2M1[nib]
    vals = vals * np.repeat(np.exp2(scales.astype(np.float64) - 127.0), 8, axis=1)[..., None]
    return vals.transpose(0, 1, 3, 2).reshape(g * 512, n)


def silu(v):
    return v / (1.0 + np.exp(-np.maximum(v, -700.0)))


K, M, T, S = 1024, 256, 1024, 512


def setup_inputs():
    n = np.random.standard_normal
    s = mx_kscale(K)[:, None]
    p_w = pack_weight(n((K, M)) / np.sqrt(K) / s, "e2m1")
    return {
        "xT": (n((K, T)) * s).astype(np.float32),
        "w_words": p_w[0],
        "w_scales": p_w[1],
        "wgt": np.repeat(np.random.uniform(0.5, 2.0, (8, S)), 16, axis=0).astype(np.float32),
        "b": (0.3 * n(256)).astype(np.float32),
        "wgo": np.repeat(np.random.uniform(0.5, 2.0, (8, S)), 16, axis=0).astype(np.float32),
        "offs": striped8(np.stack([np.random.permutation(T)[:S] for _ in range(8)])),
        "offs2": striped8(np.stack([np.random.permutation(T)[:S] for _ in range(8)])),
    }


def reference(xT, w_words, w_scales, wgt, b, wgo, offs, offs2):
    idx = unstriped8(offs)
    group = np.arange(K) % 512 // 64
    xg = f64(wgt)[np.arange(K) // 4 % 128] * f64(xT)[np.arange(K)[:, None], idx[group]]
    xT_ = mxq(xg, 0, "e4m3")
    w_ = unpack_weight(w_words, w_scales, "e2m1")
    y = w_.T @ xT_
    place = unstriped8(offs2)[np.arange(M) % 128 // 16]
    out = np.zeros((M, T))
    out[np.arange(M)[:, None], place] = f64(wgo)[np.arange(M) % 128] * (silu(y + f64(b)[:, None]))
    return out

@@ -1,0 +1,141 @@
+from contextlib import ExitStack
+
+import concourse.mybir as mybir
+
+F32 = mybir.dt.float32
+BF16 = mybir.dt.bfloat16
+I32 = mybir.dt.int32
+U32 = mybir.dt.uint32
+U16 = mybir.dt.uint16
+U8 = mybir.dt.uint8
+FP8X4 = mybir.dt.float8_e4m3fn_x4
+FP4X4 = mybir.dt.float4_e2m1fn_x4
+MULT = mybir.AluOpType.mult
+SILU = mybir.ActivationFunctionType.Silu
+
+K, M, T, S = 1024, 256, 1024, 512
+P = 128
+PACK = 4
+PASSES = K // (P * PACK)
+BLOCKS = M // P
+HALF = S // 2
+LIST_COLS = HALF // 16
+CHUNK = 128
+
+FLOPS = 2 * K * M * S
+
+
+def tile_list_hboth_silu_kernel(tc, xT, w_words, w_scales, wgt, b, wgo, offs, offs2, out):
+    nc = tc.nc
+    with ExitStack() as ctx:
+        keep = ctx.enter_context(tc.tile_pool(name="keep", bufs=1))
+        psum = ctx.enter_context(tc.psum_pool(name="psum", bufs=1))
+
+        lists_in = keep.tile([P, S // 16], U16, name="lists_in")
+        lists_out = keep.tile([P, S // 16], U16, name="lists_out")
+        wgt_sb = [keep.tile([P, HALF], F32, name=f"wgt{h}") for h in range(2)]
+        wgo_sb = keep.tile([P, S], F32, name="wgo_sb")
+        bias = keep.tile([P, BLOCKS], F32, name="bias")
+        w_sb = keep.tile([P, PASSES, 2 * M], U8, name="w_sb", align_bytes=64)
+        ws_sb = keep.tile([P, PASSES, M], U8, name="ws_sb", align_bytes=64)
+        planes = [keep.tile([P, T], F32, name=f"plane{k}") for k in range(PASSES * PACK)]
+        picked = [[keep.tile([P, PACK, HALF], F32, name=f"picked{a}{h}") for h in range(2)] for a in range(PASSES)]
+        grouped = [[keep.tile([P, HALF, PACK], BF16, name=f"grouped{a}{h}", align_bytes=64) for h in range(2)] for a in range(PASSES)]
+        codes = [[keep.tile([P, HALF], U32, name=f"codes{a}{h}", align_bytes=64) for h in range(2)] for a in range(PASSES)]
+        scales = [[keep.tile([P, HALF], U8, name=f"scales{a}{h}", align_bytes=64) for h in range(2)] for a in range(PASSES)]
+        acts = [[keep.tile([P, HALF], F32, name=f"acts{n}{h}") for h in range(2)] for n in range(BLOCKS)]
+        placed = [keep.tile([P, T], F32, name=f"placed{n}") for n in range(BLOCKS)]
+        banks = [[psum.tile([P, HALF], F32, name=f"bank{n}{h}") for h in range(2)] for n in range(BLOCKS)]
+        warm = keep.tile([P, 1], F32, name="warm")
+        warm_out = keep.tile([P, 1], F32, name="warm_out")
+
+        xs = xT.rearrange("(a p i) t -> a p i t", p=P, i=PACK)
+        nc.sync.dma_start(out=lists_in[:], in_=offs)
+        nc.scalar.dma_start(out=wgt_sb[0][:], in_=wgt[:, 0:HALF])
+        nc.sync.dma_start(out=planes[0][:], in_=xs[0, :, 0, :])
+        nc.sync.dma_start(out=wgt_sb[1][:], in_=wgt[:, HALF:S])
+        for k in range(1, PASSES * PACK):
+            nc.sync.dma_start(out=planes[k][:], in_=xs[k // PACK, :, k % PACK, :])
+
+        nc.vector.memset(warm[:], 0.0)
+        nc.scalar.activation(out=warm_out[:], in_=warm[:], func=SILU)
+        ws_words = ws_sb[:].rearrange("p a n -> p (a n)").bitcast(I32)
+        nc.vector.memset(ws_words, 0)
+        for n in range(BLOCKS):
+            nc.gpsimd.memset(placed[n][:], 0.0)
+
+        nc.sync.dma_start(out=w_sb[:], in_=w_words.rearrange("a p n -> p a n"))
+        ws_view = ws_words.rearrange("p (a n) -> p a n", a=PASSES)
+        ws_dram = w_scales.bitcast(I32).rearrange("a q n -> q a n")
+        for q in range(4):
+            nc.sync.dma_start(out=ws_view[32 * q : 32 * q + 4, :, :], in_=ws_dram[4 * q : 4 * q + 4, :, :])
+        with nc.allow_non_contiguous_dma(reason="256 bias values, one to a partition and block"):
+            nc.sync.dma_start(out=bias[:], in_=b.rearrange("(n p) -> p n", p=P))
+        nc.sync.dma_start(out=lists_out[:], in_=offs2)
+        nc.sync.dma_start(out=wgo_sb[:], in_=wgo)
+
+        def gather(k, h):
+            a, i = k // PACK, k % PACK
+            offsets = lists_in[:, h * LIST_COLS : (h + 1) * LIST_COLS]
+            nc.vector.tensor_tensor(out=picked[a][h][:, i, :], in0=planes[k][:].indirect(offsets), in1=wgt_sb[h][:], op=MULT)
+
+        def interleave(a, h, i0, i1):
+            nc.scalar.copy(out=grouped[a][h][:, :, i0:i1], in_=picked[a][h][:, i0:i1, :].rearrange("p i j -> p j i"))
+
+        def quantize(a, h):
+            nc.vector.quantize_mx(
+                out=codes[a][h][:].bitcast(FP8X4),
+                scales=scales[a][h][:],
+                in_=grouped[a][h][:].rearrange("p j i -> p (j i)"),
+            )
+
+        def multiply(n, h):
+            for c in range(HALF // CHUNK):
+                cols = slice(c * CHUNK, (c + 1) * CHUNK)
+                for a in range(PASSES):
+                    nc.tensor.matmul_mx(
+                        out=banks[n][h][:, cols],
+                        lhsT=w_sb[:, a, 2 * P * n : 2 * P * (n + 1)].bitcast(FP4X4),
+                        lhsT_scale=ws_sb[:, a, P * n : P * (n + 1)],
+                        rhs=codes[a][h][:, cols].bitcast(FP8X4),
+                        rhs_scale=scales[a][h][:, cols],
+                        start=(a == 0),
+                        stop=(a == PASSES - 1),
+                    )
+            nc.scalar.activation(out=acts[n][h][:], in_=banks[n][h][:], func=SILU, bias=bias[:, n : n + 1])
+
+        def scatter(n, h):
+            offsets = lists_out[:, h * LIST_COLS : (h + 1) * LIST_COLS]
+            nc.vector.tensor_tensor(out=placed[n][:].indirect(offsets), in0=acts[n][h][:], in1=wgo_sb[:, h * HALF : (h + 1) * HALF], op=MULT)
+
+        for k in range(PACK):
+            gather(k, 0)
+            gather(k, 1)
+        interleave(0, 0, 0, PACK)
+        interleave(0, 1, 0, PACK)
+        gather(4, 0)
+        gather(4, 1)
+        quantize(0, 0)
+        gather(5, 0)
+        interleave(1, 0, 0, 2)
+        gather(6, 0)
+        gather(5, 1)
+        interleave(1, 1, 0, 2)
+        gather(7, 0)
+        interleave(1, 0, 2, 4)
+        gather(6, 1)
+        quantize(0, 1)
+        quantize(1, 0)
+        multiply(0, 0)
+        multiply(1, 0)
+        gather(7, 1)
+        interleave(1, 1, 2, 4)
+        scatter(0, 0)
+        quantize(1, 1)
+        multiply(0, 1)
+        multiply(1, 1)
+        scatter(1, 0)
+        scatter(0, 1)
+        nc.sync.dma_start(out=out[0:P, :], in_=placed[0][:])
+        scatter(1, 1)
+        nc.sync.dma_start(out=out[P : 2 * P, :], in_=placed[1][:])

@@ -40,22 +40,25 @@ def tile_list_hboth_silu_kernel(tc, xT, w_words, w_scales, wgt, b, wgo, offs, of
         ws_sb = keep.tile([P, PASSES, M], U8, name="ws_sb", align_bytes=64)
         planes = [keep.tile([P, T], F32, name=f"plane{k}") for k in range(PASSES * PACK)]
         picked = [[keep.tile([P, PACK, HALF], F32, name=f"picked{a}{h}") for h in range(2)] for a in range(PASSES)]
-        grouped = [[keep.tile([P, HALF, PACK], BF16, name=f"grouped{a}{h}", align_bytes=64) for h in range(2)] for a in range(PASSES)]
-        codes = [[keep.tile([P, HALF], U32, name=f"codes{a}{h}", align_bytes=64) for h in range(2)] for a in range(PASSES)]
-        scales = [[keep.tile([P, HALF], U8, name=f"scales{a}{h}", align_bytes=64) for h in range(2)] for a in range(PASSES)]
+        grouped = [keep.tile([P, S, PACK], BF16, name=f"grouped{a}", align_bytes=64) for a in range(PASSES)]
+        codes = [keep.tile([P, S], U32, name=f"codes{a}", align_bytes=64) for a in range(PASSES)]
+        scales = [keep.tile([P, S], U8, name=f"scales{a}", align_bytes=64) for a in range(PASSES)]
         acts = [[keep.tile([P, HALF], F32, name=f"acts{n}{h}") for h in range(2)] for n in range(BLOCKS)]
         placed = [keep.tile([P, T], F32, name=f"placed{n}") for n in range(BLOCKS)]
-        banks = [[psum.tile([P, HALF], F32, name=f"bank{n}{h}") for h in range(2)] for n in range(BLOCKS)]
+        banks = [[[psum.tile([P, CHUNK], F32, name=f"bank{n}{h}{c}") for c in range(2)] for h in range(2)] for n in range(BLOCKS)]
         warm = keep.tile([P, 1], F32, name="warm")
         warm_out = keep.tile([P, 1], F32, name="warm_out")
 
         xs = xT.rearrange("(a p i) t -> a p i t", p=P, i=PACK)
-        nc.sync.dma_start(out=lists_in[:], in_=offs)
-        nc.scalar.dma_start(out=wgt_sb[0][:], in_=wgt[:, 0:HALF])
-        nc.sync.dma_start(out=planes[0][:], in_=xs[0, :, 0, :])
-        nc.sync.dma_start(out=wgt_sb[1][:], in_=wgt[:, HALF:S])
-        for k in range(1, PASSES * PACK):
+        def load(k):
             nc.sync.dma_start(out=planes[k][:], in_=xs[k // PACK, :, k % PACK, :])
+
+        nc.scalar.dma_start(out=wgt_sb[0][:], in_=wgt[:, 0:HALF])
+        load(0)
+        nc.sync.dma_start(out=lists_in[:], in_=offs)
+        nc.sync.dma_start(out=wgt_sb[1][:], in_=wgt[:, HALF:S])
+        for k in range(1, 5):
+            load(k)
 
         nc.vector.memset(warm[:], 0.0)
         nc.scalar.activation(out=warm_out[:], in_=warm[:], func=SILU)
@@ -64,13 +67,15 @@ def tile_list_hboth_silu_kernel(tc, xT, w_words, w_scales, wgt, b, wgo, offs, of
         for n in range(BLOCKS):
             nc.gpsimd.memset(placed[n][:], 0.0)
 
-        nc.sync.dma_start(out=w_sb[:], in_=w_words.rearrange("a p n -> p a n"))
         ws_view = ws_words.rearrange("p (a n) -> p a n", a=PASSES)
         ws_dram = w_scales.bitcast(I32).rearrange("a q n -> q a n")
         for q in range(4):
             nc.sync.dma_start(out=ws_view[32 * q : 32 * q + 4, :, :], in_=ws_dram[4 * q : 4 * q + 4, :, :])
         with nc.allow_non_contiguous_dma(reason="256 bias values, one to a partition and block"):
             nc.sync.dma_start(out=bias[:], in_=b.rearrange("(n p) -> p n", p=P))
+        for k in range(5, PASSES * PACK):
+            load(k)
+        nc.sync.dma_start(out=w_sb[:], in_=w_words.rearrange("a p n -> p a n"))
         nc.sync.dma_start(out=lists_out[:], in_=offs2)
         nc.sync.dma_start(out=wgo_sb[:], in_=wgo)
 
@@ -80,29 +85,32 @@ def tile_list_hboth_silu_kernel(tc, xT, w_words, w_scales, wgt, b, wgo, offs, of
             nc.vector.tensor_tensor(out=picked[a][h][:, i, :], in0=planes[k][:].indirect(offsets), in1=wgt_sb[h][:], op=MULT)
 
         def interleave(a, h, i0, i1):
-            nc.scalar.copy(out=grouped[a][h][:, :, i0:i1], in_=picked[a][h][:, i0:i1, :].rearrange("p i j -> p j i"))
+            nc.scalar.copy(out=grouped[a][:, h * HALF : (h + 1) * HALF, i0:i1], in_=picked[a][h][:, i0:i1, :].rearrange("p i j -> p j i"))
 
-        def quantize(a, h):
+        def quantize(a, j0, j1):
             nc.vector.quantize_mx(
-                out=codes[a][h][:].bitcast(FP8X4),
-                scales=scales[a][h][:],
-                in_=grouped[a][h][:].rearrange("p j i -> p (j i)"),
+                out=codes[a][:, j0:j1].bitcast(FP8X4),
+                scales=scales[a][:, j0:j1],
+                in_=grouped[a][:, j0:j1, :].rearrange("p j i -> p (j i)"),
             )
 
-        def multiply(n, h):
-            for c in range(HALF // CHUNK):
-                cols = slice(c * CHUNK, (c + 1) * CHUNK)
-                for a in range(PASSES):
-                    nc.tensor.matmul_mx(
-                        out=banks[n][h][:, cols],
-                        lhsT=w_sb[:, a, 2 * P * n : 2 * P * (n + 1)].bitcast(FP4X4),
-                        lhsT_scale=ws_sb[:, a, P * n : P * (n + 1)],
-                        rhs=codes[a][h][:, cols].bitcast(FP8X4),
-                        rhs_scale=scales[a][h][:, cols],
-                        start=(a == 0),
-                        stop=(a == PASSES - 1),
-                    )
-            nc.scalar.activation(out=acts[n][h][:], in_=banks[n][h][:], func=SILU, bias=bias[:, n : n + 1])
+        def multiply(n, h, a):
+            for c in range(2):
+                j = h * HALF + c * CHUNK
+                nc.tensor.matmul_mx(
+                    out=banks[n][h][c][:],
+                    lhsT=w_sb[:, a, 2 * P * n : 2 * P * (n + 1)].bitcast(FP4X4),
+                    lhsT_scale=ws_sb[:, a, P * n : P * (n + 1)],
+                    rhs=codes[a][:, j : j + CHUNK].bitcast(FP8X4),
+                    rhs_scale=scales[a][:, j : j + CHUNK],
+                    start=(a == 0),
+                    stop=(a == PASSES - 1),
+                )
+
+        def finish(n, h):
+            multiply(n, h, 1)
+            for c in range(2):
+                nc.scalar.activation(out=acts[n][h][:, c * CHUNK : (c + 1) * CHUNK], in_=banks[n][h][c][:], func=SILU, bias=bias[:, n : n + 1])
 
         def scatter(n, h):
             offsets = lists_out[:, h * LIST_COLS : (h + 1) * LIST_COLS]
@@ -115,25 +123,27 @@ def tile_list_hboth_silu_kernel(tc, xT, w_words, w_scales, wgt, b, wgo, offs, of
         interleave(0, 1, 0, PACK)
         gather(4, 0)
         gather(4, 1)
-        quantize(0, 0)
         gather(5, 0)
         interleave(1, 0, 0, 2)
         gather(6, 0)
-        gather(5, 1)
-        interleave(1, 1, 0, 2)
+        quantize(0, 0, S)
+        for h in range(2):
+            for n in range(BLOCKS):
+                multiply(n, h, 0)
         gather(7, 0)
         interleave(1, 0, 2, 4)
+        gather(5, 1)
+        interleave(1, 1, 0, 2)
+        quantize(1, 0, HALF)
+        finish(0, 0)
+        finish(1, 0)
         gather(6, 1)
-        quantize(0, 1)
-        quantize(1, 0)
-        multiply(0, 0)
-        multiply(1, 0)
         gather(7, 1)
         interleave(1, 1, 2, 4)
         scatter(0, 0)
-        quantize(1, 1)
-        multiply(0, 1)
-        multiply(1, 1)
+        quantize(1, HALF, S)
+        finish(0, 1)
+        finish(1, 1)
         scatter(1, 0)
         scatter(0, 1)
         nc.sync.dma_start(out=out[0:P, :], in_=placed[0][:])

@@ -38,12 +38,10 @@ def tile_list_hboth_silu_kernel(tc, xT, w_words, w_scales, wgt, b, wgo, offs, of
         bias = keep.tile([P, BLOCKS], F32, name="bias")
         w_sb = keep.tile([P, PASSES, 2 * M], U8, name="w_sb", align_bytes=64)
         ws_sb = keep.tile([P, PASSES, M], U8, name="ws_sb", align_bytes=64)
-        planes = [keep.tile([P, T], F32, name=f"plane{k}") for k in range(PASSES * PACK)]
-        picked = [[keep.tile([P, PACK, HALF], F32, name=f"picked{a}{h}") for h in range(2)] for a in range(PASSES)]
-        grouped = [keep.tile([P, S, PACK], BF16, name=f"grouped{a}", align_bytes=64) for a in range(PASSES)]
-        codes = [keep.tile([P, S], U32, name=f"codes{a}", align_bytes=64) for a in range(PASSES)]
-        scales = [keep.tile([P, S], U8, name=f"scales{a}", align_bytes=64) for a in range(PASSES)]
-        acts = [[keep.tile([P, HALF], F32, name=f"acts{n}{h}") for h in range(2)] for n in range(BLOCKS)]
+        planes = [keep.tile([P, T], F32, name=f"plane{k}", tag=f"plane{k}", align_bytes=64) for k in range(PASSES * PACK)]
+        picked0 = [keep.tile([P, PACK, HALF], F32, name=f"picked0{h}") for h in range(2)]
+        grouped0 = [keep.tile([P, HALF, PACK], BF16, name=f"grouped0{h}", align_bytes=64) for h in range(2)]
+        scales = [[keep.tile([P, HALF], U8, name=f"scales{a}{h}", align_bytes=64) for h in range(2)] for a in range(PASSES)]
         placed = [keep.tile([P, T], F32, name=f"placed{n}") for n in range(BLOCKS)]
         banks = [[[psum.tile([P, CHUNK], F32, name=f"bank{n}{h}{c}") for c in range(2)] for h in range(2)] for n in range(BLOCKS)]
         warm = keep.tile([P, 1], F32, name="warm")
@@ -73,79 +71,98 @@ def tile_list_hboth_silu_kernel(tc, xT, w_words, w_scales, wgt, b, wgo, offs, of
             nc.sync.dma_start(out=ws_view[32 * q : 32 * q + 4, :, :], in_=ws_dram[4 * q : 4 * q + 4, :, :])
         with nc.allow_non_contiguous_dma(reason="256 bias values, one to a partition and block"):
             nc.sync.dma_start(out=bias[:], in_=b.rearrange("(n p) -> p n", p=P))
-        for k in range(5, PASSES * PACK):
+        for k in (6, 7, 5):
             load(k)
         nc.sync.dma_start(out=w_sb[:], in_=w_words.rearrange("a p n -> p a n"))
         nc.sync.dma_start(out=lists_out[:], in_=offs2)
         nc.sync.dma_start(out=wgo_sb[:], in_=wgo)
 
-        def gather(k, h):
-            a, i = k // PACK, k % PACK
+        def gather(k, h, into):
             offsets = lists_in[:, h * LIST_COLS : (h + 1) * LIST_COLS]
-            nc.vector.tensor_tensor(out=picked[a][h][:, i, :], in0=planes[k][:].indirect(offsets), in1=wgt_sb[h][:], op=MULT)
+            nc.vector.tensor_tensor(out=into, in0=planes[k][:].indirect(offsets), in1=wgt_sb[h][:], op=MULT)
 
-        def interleave(a, h, i0, i1):
-            nc.scalar.copy(out=grouped[a][:, h * HALF : (h + 1) * HALF, i0:i1], in_=picked[a][h][:, i0:i1, :].rearrange("p i j -> p j i"))
+        def interleave(into, values):
+            nc.scalar.copy(out=into, in_=values.rearrange("p i j -> p j i"))
 
-        def quantize(a, j0, j1):
+        def quantize(a, h, codes, values):
             nc.vector.quantize_mx(
-                out=codes[a][:, j0:j1].bitcast(FP8X4),
-                scales=scales[a][:, j0:j1],
-                in_=grouped[a][:, j0:j1, :].rearrange("p j i -> p (j i)"),
+                out=codes[:].bitcast(FP8X4),
+                scales=scales[a][h][:],
+                in_=values.rearrange("p j i -> p (j i)"),
             )
 
-        def multiply(n, h, a):
+        def multiply(n, h, a, codes):
             for c in range(2):
-                j = h * HALF + c * CHUNK
+                j = c * CHUNK
                 nc.tensor.matmul_mx(
                     out=banks[n][h][c][:],
                     lhsT=w_sb[:, a, 2 * P * n : 2 * P * (n + 1)].bitcast(FP4X4),
                     lhsT_scale=ws_sb[:, a, P * n : P * (n + 1)],
-                    rhs=codes[a][:, j : j + CHUNK].bitcast(FP8X4),
-                    rhs_scale=scales[a][:, j : j + CHUNK],
+                    rhs=codes[:, j : j + CHUNK].bitcast(FP8X4),
+                    rhs_scale=scales[a][h][:, j : j + CHUNK],
                     start=(a == 0),
                     stop=(a == PASSES - 1),
                 )
 
-        def finish(n, h):
-            multiply(n, h, 1)
+        def activate(n, h, acts):
             for c in range(2):
-                nc.scalar.activation(out=acts[n][h][:, c * CHUNK : (c + 1) * CHUNK], in_=banks[n][h][c][:], func=SILU, bias=bias[:, n : n + 1])
+                nc.scalar.activation(out=acts[:, c * CHUNK : (c + 1) * CHUNK], in_=banks[n][h][c][:], func=SILU, bias=bias[:, n : n + 1])
 
-        def scatter(n, h):
+        def scatter(n, h, acts):
             offsets = lists_out[:, h * LIST_COLS : (h + 1) * LIST_COLS]
-            nc.vector.tensor_tensor(out=placed[n][:].indirect(offsets), in0=acts[n][h][:], in1=wgo_sb[:, h * HALF : (h + 1) * HALF], op=MULT)
+            nc.vector.tensor_tensor(out=placed[n][:].indirect(offsets), in0=acts[:], in1=wgo_sb[:, h * HALF : (h + 1) * HALF], op=MULT)
 
         for k in range(PACK):
-            gather(k, 0)
-            gather(k, 1)
-        interleave(0, 0, 0, PACK)
-        interleave(0, 1, 0, PACK)
-        gather(4, 0)
-        gather(4, 1)
-        gather(5, 0)
-        interleave(1, 0, 0, 2)
-        gather(6, 0)
-        quantize(0, 0, S)
+            for h in range(2):
+                gather(k, h, picked0[h][:, k, :])
         for h in range(2):
-            for n in range(BLOCKS):
-                multiply(n, h, 0)
-        gather(7, 0)
-        interleave(1, 0, 2, 4)
-        gather(5, 1)
-        interleave(1, 1, 0, 2)
-        quantize(1, 0, HALF)
-        finish(0, 0)
-        finish(1, 0)
-        gather(6, 1)
-        gather(7, 1)
-        interleave(1, 1, 2, 4)
-        scatter(0, 0)
-        quantize(1, HALF, S)
-        finish(0, 1)
-        finish(1, 1)
-        scatter(1, 0)
-        scatter(0, 1)
+            interleave(grouped0[h][:], picked0[h][:])
+
+        lo0 = keep.tile([P, 2, HALF], F32, name="lo0")
+        hi0 = keep.tile([P, 2, HALF], F32, name="hi0")
+        early1 = keep.tile([P, 2, HALF], F32, name="early1")
+        grouped10 = keep.tile([P, HALF, PACK], BF16, name="grouped10", tag="shared", align_bytes=64)
+        grouped11 = keep.tile([P, HALF, PACK], BF16, name="grouped11", align_bytes=64)
+        gather(4, 0, lo0[:, 0, :])
+        gather(6, 0, hi0[:, 0, :])
+        gather(6, 1, early1[:, 1, :])
+        codes00 = keep.tile([P, HALF], U32, name="codes00", tag="plane6", align_bytes=64)
+        quantize(0, 0, codes00, grouped0[0][:])
+        multiply(0, 0, 0, codes00)
+        multiply(1, 0, 0, codes00)
+        gather(7, 0, hi0[:, 1, :])
+        interleave(grouped10[:, :, 2:4], hi0[:])
+        gather(5, 0, lo0[:, 1, :])
+        interleave(grouped10[:, :, 0:2], lo0[:])
+        gather(5, 1, early1[:, 0, :])
+        interleave(grouped11[:, :, 1:3], early1[:])
+        codes10 = keep.tile([P, HALF], U32, name="codes10", tag="codes", align_bytes=64)
+        quantize(1, 0, codes10, grouped10[:])
+        multiply(0, 0, 1, codes10)
+        multiply(1, 0, 1, codes10)
+        acts00 = keep.tile([P, HALF], F32, name="acts00")
+        activate(0, 0, acts00)
+        late1 = keep.tile([P, 2, HALF], F32, name="late1", tag="shared", align_bytes=64)
+        gather(4, 1, late1[:, 0, :])
+        gather(7, 1, late1[:, 1, :])
+        interleave(grouped11[:, :, 0:4:3], late1[:])
+        codes01 = keep.tile([P, HALF], U32, name="codes01", tag="codes", align_bytes=64)
+        quantize(0, 1, codes01, grouped0[1][:])
+        multiply(0, 1, 0, codes01)
+        multiply(1, 1, 0, codes01)
+        acts10 = keep.tile([P, HALF], F32, name="acts10", tag="shared", align_bytes=64)
+        activate(1, 0, acts10)
+        scatter(0, 0, acts00)
+        codes11 = keep.tile([P, HALF], U32, name="codes11", align_bytes=64)
+        quantize(1, 1, codes11, grouped11[:])
+        multiply(0, 1, 1, codes11)
+        multiply(1, 1, 1, codes11)
+        acts01 = keep.tile([P, HALF], F32, name="acts01")
+        acts11 = keep.tile([P, HALF], F32, name="acts11")
+        activate(0, 1, acts01)
+        activate(1, 1, acts11)
+        scatter(1, 0, acts10)
+        scatter(0, 1, acts01)
         nc.sync.dma_start(out=out[0:P, :], in_=placed[0][:])
-        scatter(1, 1)
+        scatter(1, 1, acts11)
         nc.sync.dma_start(out=out[P : 2 * P, :], in_=placed[1][:])

@@ -55,7 +55,7 @@ def tile_list_hboth_silu_kernel(tc, xT, w_words, w_scales, wgt, b, wgo, offs, of
         load(0)
         nc.sync.dma_start(out=lists_in[:], in_=offs)
         nc.sync.dma_start(out=wgt_sb[1][:], in_=wgt[:, HALF:S])
-        for k in range(1, 5):
+        for k in (1, 2, 3, 4, 6):
             load(k)
 
         nc.vector.memset(warm[:], 0.0)
@@ -69,11 +69,11 @@ def tile_list_hboth_silu_kernel(tc, xT, w_words, w_scales, wgt, b, wgo, offs, of
         ws_dram = w_scales.bitcast(I32).rearrange("a q n -> q a n")
         for q in range(4):
             nc.sync.dma_start(out=ws_view[32 * q : 32 * q + 4, :, :], in_=ws_dram[4 * q : 4 * q + 4, :, :])
-        with nc.allow_non_contiguous_dma(reason="256 bias values, one to a partition and block"):
-            nc.sync.dma_start(out=bias[:], in_=b.rearrange("(n p) -> p n", p=P))
-        for k in (6, 7, 5):
+        for k in (7, 5):
             load(k)
         nc.sync.dma_start(out=w_sb[:], in_=w_words.rearrange("a p n -> p a n"))
+        with nc.allow_non_contiguous_dma(reason="256 bias values, one to a partition and block"):
+            nc.sync.dma_start(out=bias[:], in_=b.rearrange("(n p) -> p n", p=P))
         nc.sync.dma_start(out=lists_out[:], in_=offs2)
         nc.sync.dma_start(out=wgo_sb[:], in_=wgo)
 

from contextlib import ExitStack

import concourse.mybir as mybir

F32 = mybir.dt.float32
BF16 = mybir.dt.bfloat16
I32 = mybir.dt.int32
U32 = mybir.dt.uint32
U16 = mybir.dt.uint16
U8 = mybir.dt.uint8
FP8X4 = mybir.dt.float8_e4m3fn_x4
FP4X4 = mybir.dt.float4_e2m1fn_x4
MULT = mybir.AluOpType.mult
SILU = mybir.ActivationFunctionType.Silu

K, M, T, S = 1024, 256, 1024, 512
P = 128
PACK = 4
PASSES = K // (P * PACK)
BLOCKS = M // P
HALF = S // 2
LIST_COLS = HALF // 16
CHUNK = 128

FLOPS = 2 * K * M * S


def tile_list_hboth_silu_kernel(tc, xT, w_words, w_scales, wgt, b, wgo, offs, offs2, out):
    nc = tc.nc
    with ExitStack() as ctx:
        keep = ctx.enter_context(tc.tile_pool(name="keep", bufs=1))
        psum = ctx.enter_context(tc.psum_pool(name="psum", bufs=1))

        lists_in = keep.tile([P, S // 16], U16, name="lists_in")
        lists_out = keep.tile([P, S // 16], U16, name="lists_out")
        wgt_sb = [keep.tile([P, HALF], F32, name=f"wgt{h}") for h in range(2)]
        wgo_sb = keep.tile([P, S], F32, name="wgo_sb")
        bias = keep.tile([P, BLOCKS], F32, name="bias")
        w_sb = keep.tile([P, PASSES, 2 * M], U8, name="w_sb", align_bytes=64)
        ws_sb = keep.tile([P, PASSES, M], U8, name="ws_sb", align_bytes=64)
        planes = [keep.tile([P, T], F32, name=f"plane{k}", tag=f"plane{k}", align_bytes=64) for k in range(PASSES * PACK)]
        picked0 = [keep.tile([P, PACK, HALF], F32, name=f"picked0{h}") for h in range(2)]
        grouped0 = [keep.tile([P, HALF, PACK], BF16, name=f"grouped0{h}", align_bytes=64) for h in range(2)]
        scales = [[keep.tile([P, HALF], U8, name=f"scales{a}{h}", align_bytes=64) for h in range(2)] for a in range(PASSES)]
        placed = [keep.tile([P, T], F32, name=f"placed{n}") for n in range(BLOCKS)]
        banks = [[[psum.tile([P, CHUNK], F32, name=f"bank{n}{h}{c}") for c in range(2)] for h in range(2)] for n in range(BLOCKS)]
        warm = keep.tile([P, 1], F32, name="warm")
        warm_out = keep.tile([P, 1], F32, name="warm_out")

        xs = xT.rearrange("(a p i) t -> a p i t", p=P, i=PACK)
        def load(k):
            nc.sync.dma_start(out=planes[k][:], in_=xs[k // PACK, :, k % PACK, :])

        nc.scalar.dma_start(out=wgt_sb[0][:], in_=wgt[:, 0:HALF])
        load(0)
        nc.sync.dma_start(out=lists_in[:], in_=offs)
        nc.sync.dma_start(out=wgt_sb[1][:], in_=wgt[:, HALF:S])
        for k in (1, 2, 3, 4, 6):
            load(k)

        nc.vector.memset(warm[:], 0.0)
        nc.scalar.activation(out=warm_out[:], in_=warm[:], func=SILU)
        ws_words = ws_sb[:].rearrange("p a n -> p (a n)").bitcast(I32)
        nc.vector.memset(ws_words, 0)
        for n in range(BLOCKS):
            nc.gpsimd.memset(placed[n][:], 0.0)

        ws_view = ws_words.rearrange("p (a n) -> p a n", a=PASSES)
        ws_dram = w_scales.bitcast(I32).rearrange("a q n -> q a n")
        for q in range(4):
            nc.sync.dma_start(out=ws_view[32 * q : 32 * q + 4, :, :], in_=ws_dram[4 * q : 4 * q + 4, :, :])
        for k in (7, 5):
            load(k)
        nc.sync.dma_start(out=w_sb[:], in_=w_words.rearrange("a p n -> p a n"))
        with nc.allow_non_contiguous_dma(reason="256 bias values, one to a partition and block"):
            nc.sync.dma_start(out=bias[:], in_=b.rearrange("(n p) -> p n", p=P))
        nc.sync.dma_start(out=lists_out[:], in_=offs2)
        nc.sync.dma_start(out=wgo_sb[:], in_=wgo)

        def gather(k, h, into):
            offsets = lists_in[:, h * LIST_COLS : (h + 1) * LIST_COLS]
            nc.vector.tensor_tensor(out=into, in0=planes[k][:].indirect(offsets), in1=wgt_sb[h][:], op=MULT)

        def interleave(into, values):
            nc.scalar.copy(out=into, in_=values.rearrange("p i j -> p j i"))

        def quantize(a, h, codes, values):
            nc.vector.quantize_mx(
                out=codes[:].bitcast(FP8X4),
                scales=scales[a][h][:],
                in_=values.rearrange("p j i -> p (j i)"),
            )

        def multiply(n, h, a, codes):
            for c in range(2):
                j = c * CHUNK
                nc.tensor.matmul_mx(
                    out=banks[n][h][c][:],
                    lhsT=w_sb[:, a, 2 * P * n : 2 * P * (n + 1)].bitcast(FP4X4),
                    lhsT_scale=ws_sb[:, a, P * n : P * (n + 1)],
                    rhs=codes[:, j : j + CHUNK].bitcast(FP8X4),
                    rhs_scale=scales[a][h][:, j : j + CHUNK],
                    start=(a == 0),
                    stop=(a == PASSES - 1),
                )

        def activate(n, h, acts):
            for c in range(2):
                nc.scalar.activation(out=acts[:, c * CHUNK : (c + 1) * CHUNK], in_=banks[n][h][c][:], func=SILU, bias=bias[:, n : n + 1])

        def scatter(n, h, acts):
            offsets = lists_out[:, h * LIST_COLS : (h + 1) * LIST_COLS]
            nc.vector.tensor_tensor(out=placed[n][:].indirect(offsets), in0=acts[:], in1=wgo_sb[:, h * HALF : (h + 1) * HALF], op=MULT)

        for k in range(PACK):
            for h in range(2):
                gather(k, h, picked0[h][:, k, :])
        for h in range(2):
            interleave(grouped0[h][:], picked0[h][:])

        lo0 = keep.tile([P, 2, HALF], F32, name="lo0")
        hi0 = keep.tile([P, 2, HALF], F32, name="hi0")
        early1 = keep.tile([P, 2, HALF], F32, name="early1")
        grouped10 = keep.tile([P, HALF, PACK], BF16, name="grouped10", tag="shared", align_bytes=64)
        grouped11 = keep.tile([P, HALF, PACK], BF16, name="grouped11", align_bytes=64)
        gather(4, 0, lo0[:, 0, :])
        gather(6, 0, hi0[:, 0, :])
        gather(6, 1, early1[:, 1, :])
        codes00 = keep.tile([P, HALF], U32, name="codes00", tag="plane6", align_bytes=64)
        quantize(0, 0, codes00, grouped0[0][:])
        multiply(0, 0, 0, codes00)
        multiply(1, 0, 0, codes00)
        gather(7, 0, hi0[:, 1, :])
        interleave(grouped10[:, :, 2:4], hi0[:])
        gather(5, 0, lo0[:, 1, :])
        interleave(grouped10[:, :, 0:2], lo0[:])
        gather(5, 1, early1[:, 0, :])
        interleave(grouped11[:, :, 1:3], early1[:])
        codes10 = keep.tile([P, HALF], U32, name="codes10", tag="codes", align_bytes=64)
        quantize(1, 0, codes10, grouped10[:])
        multiply(0, 0, 1, codes10)
        multiply(1, 0, 1, codes10)
        acts00 = keep.tile([P, HALF], F32, name="acts00")
        activate(0, 0, acts00)
        late1 = keep.tile([P, 2, HALF], F32, name="late1", tag="shared", align_bytes=64)
        gather(4, 1, late1[:, 0, :])
        gather(7, 1, late1[:, 1, :])
        interleave(grouped11[:, :, 0:4:3], late1[:])
        codes01 = keep.tile([P, HALF], U32, name="codes01", tag="codes", align_bytes=64)
        quantize(0, 1, codes01, grouped0[1][:])
        multiply(0, 1, 0, codes01)
        multiply(1, 1, 0, codes01)
        acts10 = keep.tile([P, HALF], F32, name="acts10", tag="shared", align_bytes=64)
        activate(1, 0, acts10)
        scatter(0, 0, acts00)
        codes11 = keep.tile([P, HALF], U32, name="codes11", align_bytes=64)
        quantize(1, 1, codes11, grouped11[:])
        multiply(0, 1, 1, codes11)
        multiply(1, 1, 1, codes11)
        acts01 = keep.tile([P, HALF], F32, name="acts01")
        acts11 = keep.tile([P, HALF], F32, name="acts11")
        activate(0, 1, acts01)
        activate(1, 1, acts11)
        scatter(1, 0, acts10)
        scatter(0, 1, acts01)
        nc.sync.dma_start(out=out[0:P, :], in_=placed[0][:])
        scatter(1, 1, acts11)
        nc.sync.dma_start(out=out[P : 2 * P, :], in_=placed[1][:])
